import numpy as np
import ml_dtypes


def mxq(x, axis, fmt="e4m3"):
    dtype, down = {"e4m3": (ml_dtypes.float8_e4m3fn, 7), "e5m2": (ml_dtypes.float8_e5m2, 14)}[fmt]
    v = np.moveaxis(np.asarray(x, np.float32).astype(ml_dtypes.bfloat16).astype(np.float64), axis, -1)
    blocks = v.reshape(v.shape[:-1] + (-1, 32))
    amax = np.abs(blocks).max(-1, keepdims=True)
    byte = np.maximum(np.where(amax > 0, np.frexp(amax)[1] - 1 + 127, 0) - down, 1)
    scale = np.exp2(byte - 127.0)
    codes = (blocks / scale).astype(np.float32).astype(dtype).astype(np.float64)
    return np.moveaxis((codes * scale).reshape(v.shape), -1, axis)


WIDE = False


def mx_kscale(k):
    if not WIDE:
        return np.ones(k)
    levels = np.array([10, -10, 5, -5, 0])
    if k % 512:
        return np.exp2(np.random.permutation(np.resize(levels, k // 32))).repeat(32)
    a = np.empty((k // 512, 16))
    for p in range(k // 512):
        a[p, :8] = np.random.permutation(np.resize(levels, 8))
        for g in range(8):
            far = levels[np.abs(levels - a[p, g]) >= 10]
            a[p, g + 8] = far[np.random.randint(len(far))]
    return np.exp2(a.ravel()).repeat(32)


def f64(x):
    return np.asarray(x).astype(np.float64)


def striped(idx):
    return np.tile(idx.reshape(-1, 16).T, (8, 1)).astype(np.uint16)


def unstriped(offs):
    return offs[:16].T.reshape(-1).astype(np.int64)


E2M1 = np.array([0.0, 0.5, 1.0, 1.5, 2.0, 3.0, 4.0, 6.0, -0.0, -0.5, -1.0, -1.5, -2.0, -3.0, -4.0, -6.0])


def pack_weight(w, fmt):
    k, n = w.shape
    w = f64(np.asarray(w, np.float32).astype(ml_dtypes.bfloat16)).reshape(k // 32, 32, n)
    amax = np.abs(w).max(1)
    if fmt == "e4m3":
        byte = np.frexp(amax)[1] - 1 + 127 - 7
    else:
        mant, ex = np.frexp(amax / 6.0)
        byte = np.where(mant > 0.5, ex, ex - 1) + 127
    byte = np.clip(np.where(amax > 0, byte, 1), 1, 254)
    scaled = (w * np.exp2(127.0 - byte)[:, None, :]).reshape(k, n).astype(np.float32)
    by_word = np.ascontiguousarray(scaled.reshape(k // 512, 128, 4, n).transpose(0, 1, 3, 2))
    if fmt == "e4m3":
        words = by_word.astype(ml_dtypes.float8_e4m3fn).view(np.uint8)
    else:
        c = by_word.astype(ml_dtypes.float4_e2m1fn).view(np.uint8) & 0xF
        words = (c[..., 0::2] | (c[..., 1::2] << 4)).reshape(k // 512, 128, 2 * n)
    return np.ascontiguousarray(words), np.ascontiguousarray(byte.astype(np.uint8).reshape(k // 512, 16, n))


def unpack_weight(words, scales, fmt):
    g, _, n = scales.shape
    words = np.ascontiguousarray(words).reshape(g, 128, n, -1)
    if fmt == "e4m3":
        vals = words.view(ml_dtypes.float8_e4m3fn).astype(np.float64)
    else:
        nib = np.empty((g, 128, n, 4), np.uint8)
        nib[..., 0::2] = words & 0xF
        nib[..., 1::2] = words >> 4
        vals = E2M1[nib]
    vals = vals * np.repeat(np.exp2(scales.astype(np.float64) - 127.0), 8, axis=1)[..., None]
    return vals.transpose(0, 1, 3, 2).reshape(g * 512, n)


def gelu(v):
    return 0.5 * v * (1.0 + np.tanh(np.sqrt(2.0 / np.pi) * (v + 0.044715 * v**3)))


K, T, S, H, P = 512, 4096, 1024, 1024, 512

def setup_inputs():
    n = np.random.standard_normal
    s = mx_kscale(K)[:, None]
    u = mx_kscale(H)[:, None]
    tab_words, tab_scales = pack_weight(n((K, T)) * s, "e4m3")
    w4_words, w4_scales = pack_weight(0.5 * n((K, H)) / np.sqrt(K) / s, "e2m1")
    return {
        "tab_words": tab_words,
        "tab_scales": tab_scales,
        "offs": striped(np.random.permutation(T)[:S]),
        "w1": (1.5 * n((K, H)) / np.sqrt(K) / s).astype(np.float32),
        "w4_words": w4_words,
        "w4_scales": w4_scales,
        "gain": (np.exp(0.3 * n(H)) * u[:, 0]).astype(np.float32),
        "pos1": striped(np.random.permutation(S)[:P]),
        "base": (0.7 * n((H, P)) * u).astype(np.float32),
        "w2": (1.6 * n((H, H)) / np.sqrt(H) / u).astype(np.float32),
        "skip": (np.exp(0.3 * n(H)) / u[:, 0]).astype(np.float32),
        "wgo": np.exp(0.3 * n((128, P))).astype(np.float32),
    }

def reference(tab_words, tab_scales, offs, w1, w4_words, w4_scales, gain, pos1, base, w2, skip, wgo):
    v = unpack_weight(tab_words, tab_scales, "e4m3")[:, unstriped(offs)]
    w4 = unpack_weight(w4_words, w4_scales, "e2m1")
    a = mxq(f64(w1), 0, "e4m3").T @ v
    b = w4.T @ v
    h = f64(gain)[:, None] * ((np.tanh(a) + b) * np.cos(b))
    x = mxq(np.maximum(h[:, unstriped(pos1)], f64(base)), 0, "e4m3")
    y = np.tanh(mxq(f64(w2), 0, "e4m3").T @ x)
    out = f64(skip)[:, None] * h
    out[:, unstriped(pos1)] = np.tile(f64(wgo), (H // 128, 1)) * y
    return out

@@ -1,0 +1,191 @@
+import math
+from contextlib import ExitStack
+
+import concourse.mybir as mybir
+
+K, T, S, H, E = 512, 4096, 1024, 1024, 512
+FLOPS = 2 * (2 * K * H * S + H * H * E)
+
+F32 = mybir.dt.float32
+BF16 = mybir.dt.bfloat16
+I32 = mybir.dt.int32
+U32 = mybir.dt.uint32
+U16 = mybir.dt.uint16
+U8 = mybir.dt.uint8
+FP8X4 = mybir.dt.float8_e4m3fn_x4
+FP4X4 = mybir.dt.float4_e2m1fn_x4
+ACT = mybir.ActivationFunctionType
+ALU = mybir.AluOpType
+
+P = 128
+PACK = 4
+GROUP = P * PACK
+BANK = 512
+GROUPS = H // GROUP
+HALVES = S // BANK
+
+
+def tile_list_lens_edge_refiner_kernel(
+    tc, tab_words, tab_scales, offs, w1, w4_words, w4_scales, gain, pos1, base, w2, skip, wgo, out
+):
+    nc = tc.nc
+    with ExitStack() as ctx:
+        keep = ctx.enter_context(tc.tile_pool(name="keep", bufs=1))
+        work = ctx.enter_context(tc.tile_pool(name="work", bufs=2))
+        psum = ctx.enter_context(tc.psum_pool(name="psum", bufs=4))
+
+        offs_sb = keep.tile([P, S // 16], U16, name="offs_sb")
+        pos_sb = keep.tile([P, E // 16], U16, name="pos_sb")
+        tab_w = keep.tile([P, T], U32, name="tab_w", align_bytes=64)
+        tab_s = keep.tile([P, T], U8, name="tab_s", align_bytes=64)
+        w4_raw = keep.tile([P, 2 * H], U8, name="w4_raw", align_bytes=64)
+        w4s_raw = keep.tile([P, H], U8, name="w4s_raw", align_bytes=64)
+        w4_c = keep.tile([P, 2 * H], U8, name="w4_c", align_bytes=64)
+        w4_s = keep.tile([P, H], U8, name="w4_s", align_bytes=64)
+        gain_sb = keep.tile([P, GROUPS, PACK], F32, name="gain_sb")
+        skip_sb = keep.tile([P, GROUPS, PACK], F32, name="skip_sb")
+        wgo_sb = keep.tile([P, PACK, E], F32, name="wgo_sb")
+
+        nc.gpsimd.memset(w4s_raw[:].bitcast(I32), 0)
+
+        nc.vector.memset(tab_s[:].bitcast(I32), 0)
+
+        def load_rows(src, tag, bufs):
+            raw = work.tile([P, PACK, BANK], F32, name=tag, tag=tag, bufs=bufs)
+            nc.sync.dma_start(raw[:], src.rearrange("(p j) c -> p j c", j=PACK))
+            return raw
+
+        for q in range(4):
+            nc.sync.dma_start(w4s_raw[32 * q : 32 * q + 4, :].bitcast(I32), w4_scales[0, 4 * q : 4 * q + 4, :].bitcast(I32))
+        w1_raw = [load_rows(w1[:, 0:GROUP], "w_raw", 4)]
+        nc.sync.dma_start(offs_sb[:], offs)
+        for q in range(4):
+            nc.sync.dma_start(tab_s[32 * q : 32 * q + 4, :].bitcast(I32), tab_scales[0, 4 * q : 4 * q + 4, :].bitcast(I32))
+        nc.sync.dma_start(w4_raw[:].bitcast(I32), w4_words[0].bitcast(I32))
+        nc.sync.dma_start(tab_w[:].bitcast(I32), tab_words[0].rearrange("p t i -> p (t i)").bitcast(I32))
+        w1_raw.append(load_rows(w1[:, GROUP : 2 * GROUP], "w_raw", 4))
+        nc.sync.dma_start(gain_sb[:], gain.rearrange("(g p t) -> p g t", g=GROUPS, t=PACK))
+        nc.sync.dma_start(pos_sb[:], pos1)
+        base_sb = [load_rows(base[g * GROUP : (g + 1) * GROUP, :], "base_sb", 2) for g in range(GROUPS)]
+        w2_raw = {}
+        for g in range(GROUPS):
+            for a in range(GROUPS):
+                w2_raw[g, a] = load_rows(w2[a * GROUP : (a + 1) * GROUP, g * GROUP : (g + 1) * GROUP], "w_raw", 4)
+        nc.sync.dma_start(skip_sb[:], skip.rearrange("(g p t) -> p g t", g=GROUPS, t=PACK))
+        for u in range(4):
+            nc.sync.dma_start(wgo_sb[32 * u : 32 * u + 32], wgo.rearrange("(p t) m -> p t m", t=PACK))
+
+        v_w = [keep.tile([P, BANK], U32, name=f"v_w{c}", align_bytes=64) for c in range(HALVES)]
+        v_s = [keep.tile([P, BANK], U8, name=f"v_s{c}", align_bytes=64) for c in range(HALVES)]
+        cols = BANK // 16
+        for c in range(HALVES):
+            nc.vector.tensor_copy(v_s[c][:], tab_s[:].indirect(offs_sb[:, c * cols : (c + 1) * cols]))
+        nc.vector.tensor_copy(
+            w4_c[:].bitcast(U16).rearrange("p (g t m) -> p g m t", g=GROUPS, t=PACK),
+            w4_raw[:].bitcast(U16).rearrange("p (g m t) -> p g m t", g=GROUPS, t=PACK),
+        )
+        nc.vector.tensor_copy(
+            w4_s[:].rearrange("p (g t m) -> p g t m", g=GROUPS, t=PACK),
+            w4s_raw[:].rearrange("p (g m t) -> p g t m", g=GROUPS, t=PACK),
+        )
+        for c in range(HALVES):
+            nc.vector.tensor_copy(v_w[c][:], tab_w[:].indirect(offs_sb[:, c * cols : (c + 1) * cols]))
+
+        def round_weight(raw, tag, copy=nc.scalar.copy):
+            grouped = work.tile([P, GROUP * PACK], BF16, name="grouped", tag=tag, bufs=3 if tag == "cosb" else 1, align_bytes=64)
+            dst = grouped[:].rearrange("p (t m j) -> p m j t", t=PACK, j=PACK)
+            src = raw[:].rearrange("p j (m t) -> p m j t", t=PACK)
+            copy(dst, src)
+            return grouped
+
+        def quantize(grouped, name):
+            codes = keep.tile([P, BANK], U32, name=name + "_c", align_bytes=64)
+            scales = keep.tile([P, BANK], U8, name=name + "_s", align_bytes=64)
+            nc.vector.quantize_mx(out=codes[:].bitcast(FP8X4), scales=scales[:], in_=grouped[:])
+            return codes, scales
+
+        w1_q = {0: quantize(round_weight(w1_raw[0], "grouped"), "w1q0")}
+        w2_q = {}
+        x_q = {}
+        h = {}
+        picked = {}
+
+        def features(g, t):
+            w1_c, w1_s = w1_q[g]
+            m = slice(t * P, (t + 1) * P)
+            n0 = g * GROUP + t * P
+            absb = work.tile([P, S], F32, name="absb", tag="absb", bufs=1, align_bytes=64)
+            cosb = work.tile([P, S], F32, name="cosb", tag="cosb", bufs=3, align_bytes=64)
+            summ = work.tile([P, S], F32, name="summ", tag="summ", bufs=3, align_bytes=64)
+            for c in range(HALVES):
+                j = slice(c * BANK, (c + 1) * BANK)
+                b_ps = psum.tile([P, BANK], F32, name="b_ps", bufs=6)
+                a_ps = psum.tile([P, BANK], F32, name="a_ps", bufs=2)
+                nc.tensor.matmul_mx(b_ps[:], lhsT=w4_c[:, 2 * n0 : 2 * (n0 + P)].bitcast(FP4X4), lhsT_scale=w4_s[:, n0 : n0 + P],
+                                    rhs=v_w[c][:].bitcast(FP8X4), rhs_scale=v_s[c][:], start=True, stop=True)
+                nc.tensor.matmul_mx(a_ps[:], lhsT=w1_c[:, m].bitcast(FP8X4), lhsT_scale=w1_s[:, m],
+                                    rhs=v_w[c][:].bitcast(FP8X4), rhs_scale=v_s[c][:], start=True, stop=True)
+                nc.scalar.activation(absb[:, j], b_ps[:], ACT.Abs)
+                nc.scalar.activation(summ[:, j], a_ps[:], ACT.Tanh)
+                nc.vector.tensor_tensor(summ[:, j], b_ps[:], summ[:, j], ALU.add)
+            nc.scalar.activation(cosb[:], absb[:], ACT.Sin, bias=math.pi / 2, scale=-1.0)
+            h[g, t] = keep.tile([P, S], F32, name=f"h{g}{t}")
+            nc.vector.scalar_tensor_tensor(h[g, t][:], cosb[:], gain_sb[:, g, t : t + 1], summ[:], ALU.mult, ALU.mult)
+
+        def pick(g, t):
+            if t == 0:
+                picked[g] = work.tile([P, PACK, E], F32, name="picked")
+            nc.vector.tensor_copy(picked[g][:, t, :], h[g, t][:].indirect(pos_sb[:]))
+
+        def edge_operand(g):
+            grouped = work.tile([P, E * PACK], BF16, name="x_grouped", tag="x_grouped", bufs=1, align_bytes=64)
+            nc.vector.tensor_tensor(
+                grouped[:].rearrange("p (c i t) -> p c t i", i=4, t=PACK),
+                picked[g][:].rearrange("p t (c i) -> p c t i", i=4),
+                base_sb[g][:].rearrange("p t (c i) -> p c t i", i=4),
+                ALU.max,
+            )
+            return grouped
+
+        tiles = [(g, t) for g in range(GROUPS) for t in range(PACK)]
+        x_grouped = {}
+        w_grouped = {}
+        for i, (g, t) in enumerate(tiles):
+            features(g, t)
+            if i > 0:
+                pick(*tiles[i - 1])
+            if i == 0:
+                w_grouped["w1"] = round_weight(w1_raw[1], "grouped", nc.vector.tensor_copy)
+            if i == 1:
+                w1_q[1] = quantize(w_grouped["w1"], "w1q1")
+            if i == 4:
+                x_grouped[0] = edge_operand(0)
+            if i == 5:
+                x_q[0] = quantize(x_grouped[0], "xq0")
+        w_grouped[0, 0] = round_weight(w2_raw[0, 0], "absb")
+        w_grouped[0, 1] = round_weight(w2_raw[0, 1], "cosb")
+        pick(*tiles[-1])
+        x_grouped[1] = edge_operand(1)
+        w2_q[0, 0] = quantize(w_grouped[0, 0], "w2q00")
+        x_q[1] = quantize(x_grouped[1], "xq1")
+        w2_q[0, 1] = quantize(w_grouped[0, 1], "w2q01")
+
+        for i, (g, t) in enumerate(tiles):
+            m = slice(t * P, (t + 1) * P)
+            y_ps = psum.tile([P, BANK], F32, name="a_ps", bufs=2)
+            for a in range(GROUPS):
+                w2_c, w2_s = w2_q[g, a]
+                x_c, x_s = x_q[a]
+                nc.tensor.matmul_mx(y_ps[:], lhsT=w2_c[:, m].bitcast(FP8X4), lhsT_scale=w2_s[:, m],
+                                    rhs=x_c[:].bitcast(FP8X4), rhs_scale=x_s[:], start=(a == 0), stop=(a == GROUPS - 1))
+            page = work.tile([P, S], F32, name="page", tag=("cosb", "summ")[i % 2], bufs=3, align_bytes=64)
+            nc.scalar.activation(page[:], h[g, t][:], ACT.Copy, scale=skip_sb[:, g, t : t + 1])
+            y = work.tile([P, E], F32, name="y", bufs=3)
+            nc.scalar.activation(y[:], y_ps[:], ACT.Tanh)
+            if i in (0, 1):
+                w_grouped[1, i] = round_weight(w2_raw[1, i], ("absb", "x_grouped")[i])
+            nc.vector.tensor_tensor(page[:].indirect(pos_sb[:]), y[:], wgo_sb[:, t, :], ALU.mult)
+            if i in (1, 2):
+                w2_q[1, i - 1] = quantize(w_grouped[1, i - 1], f"w2q1{i - 1}")
+            rows = out[g * GROUP : (g + 1) * GROUP, :].rearrange("(p t) j -> p t j", t=PACK)
+            nc.sync.dma_start(rows[:, t, :], page[:])

@@ -23,6 +23,14 @@ GROUP = P * PACK
 BANK = 512
 GROUPS = H // GROUP
 HALVES = S // BANK
+BANK_BYTES = 4 * BANK
+SLOT_BYTES = 4 * S
+RING = 3
+ABS_SLOT, W1_SLOT, X_SLOT = 0, 1, 2
+COS_SLOT = 3
+SUM_SLOT = COS_SLOT + RING
+PICK_SLOT = SUM_SLOT + RING
+A_BANKS, B_BANKS = 2, 6
 
 
 def tile_list_lens_edge_refiner_kernel(
@@ -32,7 +40,15 @@ def tile_list_lens_edge_refiner_kernel(
     with ExitStack() as ctx:
         keep = ctx.enter_context(tc.tile_pool(name="keep", bufs=1))
         work = ctx.enter_context(tc.tile_pool(name="work", bufs=2))
-        psum = ctx.enter_context(tc.psum_pool(name="psum", bufs=4))
+        psum = ctx.enter_context(tc.psum_pool(name="psum", bufs=1))
+        slots = ctx.enter_context(tc.tile_pool(name="slots", bufs=1))
+
+        def in_slot(slot, shape, dtype, name):
+            return slots.tile(shape, dtype, name=name, offset=slot * SLOT_BYTES, align_bytes=64)
+
+        def in_bank(bank, width, name):
+            return psum.tile([P, width], F32, name=name, offset=bank * BANK_BYTES)
+
 
         offs_sb = keep.tile([P, S // 16], U16, name="offs_sb")
         pos_sb = keep.tile([P, E // 16], U16, name="pos_sb")
@@ -47,6 +63,10 @@ def tile_list_lens_edge_refiner_kernel(
         wgo_sb = keep.tile([P, PACK, E], F32, name="wgo_sb")
 
         nc.gpsimd.memset(w4s_raw[:].bitcast(I32), 0)
+        warm_in = keep.tile([P, 1], F32, name="warm_in")
+        warm_out = keep.tile([P, 1], F32, name="warm_out")
+        nc.gpsimd.memset(warm_in[:], 0.0)
+        nc.scalar.activation(warm_out[:], warm_in[:], ACT.Silu)
 
         nc.vector.memset(tab_s[:].bitcast(I32), 0)
 
@@ -91,20 +111,28 @@ def tile_list_lens_edge_refiner_kernel(
         for c in range(HALVES):
             nc.vector.tensor_copy(v_w[c][:], tab_w[:].indirect(offs_sb[:, c * cols : (c + 1) * cols]))
 
-        def round_weight(raw, tag, copy=nc.scalar.copy):
-            grouped = work.tile([P, GROUP * PACK], BF16, name="grouped", tag=tag, bufs=3 if tag == "cosb" else 1, align_bytes=64)
+        def round_weight(raw, slot, name, copy=nc.scalar.copy):
+            grouped = in_slot(slot, [P, GROUP * PACK], BF16, name)
             dst = grouped[:].rearrange("p (t m j) -> p m j t", t=PACK, j=PACK)
             src = raw[:].rearrange("p j (m t) -> p m j t", t=PACK)
             copy(dst, src)
             return grouped
 
-        def quantize(grouped, name):
+        def mx_tiles(name):
             codes = keep.tile([P, BANK], U32, name=name + "_c", align_bytes=64)
             scales = keep.tile([P, BANK], U8, name=name + "_s", align_bytes=64)
-            nc.vector.quantize_mx(out=codes[:].bitcast(FP8X4), scales=scales[:], in_=grouped[:])
             return codes, scales
 
-        w1_q = {0: quantize(round_weight(w1_raw[0], "grouped"), "w1q0")}
+        def quantize_columns(grouped, dst, m):
+            codes, scales = dst
+            nc.vector.quantize_mx(out=codes[:, m].bitcast(FP8X4), scales=scales[:, m], in_=grouped[:, PACK * m.start : PACK * m.stop])
+
+        def quantize(grouped, name):
+            dst = mx_tiles(name)
+            quantize_columns(grouped, dst, slice(0, BANK))
+            return dst
+
+        w1_q = {0: quantize(round_weight(w1_raw[0], W1_SLOT, "w1g0"), "w1q0")}
         w2_q = {}
         x_q = {}
         h = {}
@@ -114,13 +142,14 @@ def tile_list_lens_edge_refiner_kernel(
             w1_c, w1_s = w1_q[g]
             m = slice(t * P, (t + 1) * P)
             n0 = g * GROUP + t * P
-            absb = work.tile([P, S], F32, name="absb", tag="absb", bufs=1, align_bytes=64)
-            cosb = work.tile([P, S], F32, name="cosb", tag="cosb", bufs=3, align_bytes=64)
-            summ = work.tile([P, S], F32, name="summ", tag="summ", bufs=3, align_bytes=64)
+            i = g * PACK + t
+            absb = in_slot(ABS_SLOT, [P, S], F32, f"abs{i}")
+            cosb = in_slot(COS_SLOT + i % RING, [P, S], F32, f"cos{i}")
+            summ = in_slot(SUM_SLOT + i % RING, [P, S], F32, f"sum{i}")
             for c in range(HALVES):
                 j = slice(c * BANK, (c + 1) * BANK)
-                b_ps = psum.tile([P, BANK], F32, name="b_ps", bufs=6)
-                a_ps = psum.tile([P, BANK], F32, name="a_ps", bufs=2)
+                b_ps = in_bank(A_BANKS + (HALVES * i + c) % B_BANKS, BANK, f"b{i}{c}")
+                a_ps = in_bank(c, BANK, f"a{i}{c}")
                 nc.tensor.matmul_mx(b_ps[:], lhsT=w4_c[:, 2 * n0 : 2 * (n0 + P)].bitcast(FP4X4), lhsT_scale=w4_s[:, n0 : n0 + P],
                                     rhs=v_w[c][:].bitcast(FP8X4), rhs_scale=v_s[c][:], start=True, stop=True)
                 nc.tensor.matmul_mx(a_ps[:], lhsT=w1_c[:, m].bitcast(FP8X4), lhsT_scale=w1_s[:, m],
@@ -134,57 +163,61 @@ def tile_list_lens_edge_refiner_kernel(
 
         def pick(g, t):
             if t == 0:
-                picked[g] = work.tile([P, PACK, E], F32, name="picked")
+                picked[g] = in_slot(PICK_SLOT + 2 * g, [P, PACK, E], F32, f"picked{g}")
             nc.vector.tensor_copy(picked[g][:, t, :], h[g, t][:].indirect(pos_sb[:]))
 
-        def edge_operand(g):
-            grouped = work.tile([P, E * PACK], BF16, name="x_grouped", tag="x_grouped", bufs=1, align_bytes=64)
-            nc.vector.tensor_tensor(
-                grouped[:].rearrange("p (c i t) -> p c t i", i=4, t=PACK),
-                picked[g][:].rearrange("p t (c i) -> p c t i", i=4),
-                base_sb[g][:].rearrange("p t (c i) -> p c t i", i=4),
-                ALU.max,
-            )
-            return grouped
+        def edge_operand(g, parts):
+            grouped = in_slot(X_SLOT, [P, E * PACK], BF16, f"xg{g}")
+            x_q[g] = mx_tiles(f"xq{g}")
+            for m in parts:
+                nc.vector.tensor_tensor(
+                    grouped[:, PACK * m.start : PACK * m.stop].rearrange("p (c i t) -> p c t i", i=4, t=PACK),
+                    picked[g][:, :, m].rearrange("p t (c i) -> p c t i", i=4),
+                    base_sb[g][:, :, m].rearrange("p t (c i) -> p c t i", i=4),
+                    ALU.max,
+                )
+                quantize_columns(grouped, x_q[g], m)
 
+        whole = [slice(0, E)]
+        halves = [slice(0, E // 2), slice(E // 2, E)]
         tiles = [(g, t) for g in range(GROUPS) for t in range(PACK)]
-        x_grouped = {}
         w_grouped = {}
         for i, (g, t) in enumerate(tiles):
             features(g, t)
             if i > 0:
                 pick(*tiles[i - 1])
             if i == 0:
-                w_grouped["w1"] = round_weight(w1_raw[1], "grouped", nc.vector.tensor_copy)
+                w_grouped["w1"] = round_weight(w1_raw[1], W1_SLOT, "w1g1", nc.vector.tensor_copy)
             if i == 1:
                 w1_q[1] = quantize(w_grouped["w1"], "w1q1")
             if i == 4:
-                x_grouped[0] = edge_operand(0)
-            if i == 5:
-                x_q[0] = quantize(x_grouped[0], "xq0")
-        w_grouped[0, 0] = round_weight(w2_raw[0, 0], "absb")
-        w_grouped[0, 1] = round_weight(w2_raw[0, 1], "cosb")
+                edge_operand(0, whole)
+                w_grouped[0, 0] = round_weight(w2_raw[0, 0], PICK_SLOT, "w2g00")
+            if i == 6:
+                w2_q[0, 0] = quantize(w_grouped[0, 0], "w2q00")
+        w_grouped[0, 1] = round_weight(w2_raw[0, 1], ABS_SLOT, "w2g01")
         pick(*tiles[-1])
-        x_grouped[1] = edge_operand(1)
-        w2_q[0, 0] = quantize(w_grouped[0, 0], "w2q00")
-        x_q[1] = quantize(x_grouped[1], "xq1")
         w2_q[0, 1] = quantize(w_grouped[0, 1], "w2q01")
+        edge_operand(1, halves)
 
+        next_bank = [0, 1, 4, 5, 0, 1, 4, 5, 0]
         for i, (g, t) in enumerate(tiles):
-            m = slice(t * P, (t + 1) * P)
-            y_ps = psum.tile([P, BANK], F32, name="a_ps", bufs=2)
-            for a in range(GROUPS):
-                w2_c, w2_s = w2_q[g, a]
-                x_c, x_s = x_q[a]
-                nc.tensor.matmul_mx(y_ps[:], lhsT=w2_c[:, m].bitcast(FP8X4), lhsT_scale=w2_s[:, m],
-                                    rhs=x_c[:].bitcast(FP8X4), rhs_scale=x_s[:], start=(a == 0), stop=(a == GROUPS - 1))
-            page = work.tile([P, S], F32, name="page", tag=("cosb", "summ")[i % 2], bufs=3, align_bytes=64)
+            n = slice(t * P, (t + 1) * P)
+            page = in_slot((COS_SLOT, SUM_SLOT)[i % 2] + (1 + i // 2) % RING, [P, S], F32, f"page{i}")
             nc.scalar.activation(page[:], h[g, t][:], ACT.Copy, scale=skip_sb[:, g, t : t + 1])
-            y = work.tile([P, E], F32, name="y", bufs=3)
-            nc.scalar.activation(y[:], y_ps[:], ACT.Tanh)
+            for m in halves if i == 0 else whole:
+                width = m.stop - m.start
+                y_ps = in_bank(next_bank.pop(0), width, f"y{i}_{m.start}")
+                for a in range(GROUPS):
+                    w2_c, w2_s = w2_q[g, a]
+                    x_c, x_s = x_q[a]
+                    nc.tensor.matmul_mx(y_ps[:], lhsT=w2_c[:, n].bitcast(FP8X4), lhsT_scale=w2_s[:, n],
+                                        rhs=x_c[:, m].bitcast(FP8X4), rhs_scale=x_s[:, m], start=(a == 0), stop=(a == GROUPS - 1))
+                y = work.tile([P, width], F32, name="y", bufs=3)
+                nc.scalar.activation(y[:], y_ps[:], ACT.Tanh)
+                nc.vector.tensor_tensor(page[:].indirect(pos_sb[:, m.start // 16 : m.stop // 16]), y[:], wgo_sb[:, t, m], ALU.mult)
             if i in (0, 1):
-                w_grouped[1, i] = round_weight(w2_raw[1, i], ("absb", "x_grouped")[i])
-            nc.vector.tensor_tensor(page[:].indirect(pos_sb[:]), y[:], wgo_sb[:, t, :], ALU.mult)
+                w_grouped[1, i] = round_weight(w2_raw[1, i], PICK_SLOT + 2 + i, f"w2g1{i}")
             if i in (1, 2):
                 w2_q[1, i - 1] = quantize(w_grouped[1, i - 1], f"w2q1{i - 1}")
             rows = out[g * GROUP : (g + 1) * GROUP, :].rearrange("(p t) j -> p t j", t=PACK)

@@ -143,7 +143,13 @@ def tile_list_lens_edge_refiner_kernel(
             m = slice(t * P, (t + 1) * P)
             n0 = g * GROUP + t * P
             i = g * PACK + t
-            absb = in_slot(ABS_SLOT, [P, S], F32, f"abs{i}")
+            if i == 0:
+                absb = in_slot(ABS_SLOT, [P, S], F32, "abs0")
+            else:
+                gp, tp = divmod(i - 1, PACK)
+                if tp == 0:
+                    picked[gp] = in_slot(PICK_SLOT + PACK * gp, [P, PACK, S], F32, f"picked{gp}")
+                absb = picked[gp][:, tp, :]
             cosb = in_slot(COS_SLOT + i % RING, [P, S], F32, f"cos{i}")
             summ = in_slot(SUM_SLOT + i % RING, [P, S], F32, f"sum{i}")
             for c in range(HALVES):
@@ -157,23 +163,23 @@ def tile_list_lens_edge_refiner_kernel(
                 nc.scalar.activation(absb[:, j], b_ps[:], ACT.Abs)
                 nc.scalar.activation(summ[:, j], a_ps[:], ACT.Tanh)
                 nc.vector.tensor_tensor(summ[:, j], b_ps[:], summ[:, j], ALU.add)
-            nc.scalar.activation(cosb[:], absb[:], ACT.Sin, bias=math.pi / 2, scale=-1.0)
+            nc.scalar.activation(cosb[:], absb[:, :], ACT.Sin, bias=math.pi / 2, scale=-1.0)
+            if i > 0:
+                pick(*divmod(i - 1, PACK))
             h[g, t] = keep.tile([P, S], F32, name=f"h{g}{t}")
             nc.vector.scalar_tensor_tensor(h[g, t][:], cosb[:], gain_sb[:, g, t : t + 1], summ[:], ALU.mult, ALU.mult)
 
         def pick(g, t):
-            if t == 0:
-                picked[g] = in_slot(PICK_SLOT + 2 * g, [P, PACK, E], F32, f"picked{g}")
-            nc.vector.tensor_copy(picked[g][:, t, :], h[g, t][:].indirect(pos_sb[:]))
+            nc.vector.tensor_copy(picked[g][:, t, 0:E], h[g, t][:].indirect(pos_sb[:]))
 
         def edge_operand(g, parts):
             grouped = in_slot(X_SLOT, [P, E * PACK], BF16, f"xg{g}")
             x_q[g] = mx_tiles(f"xq{g}")
             for m in parts:
                 nc.vector.tensor_tensor(
-                    grouped[:, PACK * m.start : PACK * m.stop].rearrange("p (c i t) -> p c t i", i=4, t=PACK),
-                    picked[g][:, :, m].rearrange("p t (c i) -> p c t i", i=4),
-                    base_sb[g][:, :, m].rearrange("p t (c i) -> p c t i", i=4),
+                    grouped[:, PACK * m.start : PACK * m.stop].rearrange("p (c i t) -> p c t i", i=2, t=PACK),
+                    picked[g][:, :, m].rearrange("p t (c i) -> p c t i", i=2),
+                    base_sb[g][:, :, m].rearrange("p t (c i) -> p c t i", i=2),
                     ALU.max,
                 )
                 quantize_columns(grouped, x_q[g], m)
@@ -184,8 +190,6 @@ def tile_list_lens_edge_refiner_kernel(
         w_grouped = {}
         for i, (g, t) in enumerate(tiles):
             features(g, t)
-            if i > 0:
-                pick(*tiles[i - 1])
             if i == 0:
                 w_grouped["w1"] = round_weight(w1_raw[1], W1_SLOT, "w1g1", nc.vector.tensor_copy)
             if i == 1:
@@ -195,7 +199,7 @@ def tile_list_lens_edge_refiner_kernel(
                 w_grouped[0, 0] = round_weight(w2_raw[0, 0], PICK_SLOT, "w2g00")
             if i == 6:
                 w2_q[0, 0] = quantize(w_grouped[0, 0], "w2q00")
-        w_grouped[0, 1] = round_weight(w2_raw[0, 1], ABS_SLOT, "w2g01")
+        w_grouped[0, 1] = round_weight(w2_raw[0, 1], COS_SLOT, "w2g01")
         pick(*tiles[-1])
         w2_q[0, 1] = quantize(w_grouped[0, 1], "w2q01")
         edge_operand(1, halves)
@@ -217,7 +221,7 @@ def tile_list_lens_edge_refiner_kernel(
                 nc.scalar.activation(y[:], y_ps[:], ACT.Tanh)
                 nc.vector.tensor_tensor(page[:].indirect(pos_sb[:, m.start // 16 : m.stop // 16]), y[:], wgo_sb[:, t, m], ALU.mult)
             if i in (0, 1):
-                w_grouped[1, i] = round_weight(w2_raw[1, i], PICK_SLOT + 2 + i, f"w2g1{i}")
+                w_grouped[1, i] = round_weight(w2_raw[1, i], PICK_SLOT + PACK + i, f"w2g1{i}")
             if i in (1, 2):
                 w2_q[1, i - 1] = quantize(w_grouped[1, i - 1], f"w2q1{i - 1}")
             rows = out[g * GROUP : (g + 1) * GROUP, :].rearrange("(p t) j -> p t j", t=PACK)

@@ -26,6 +26,7 @@ HALVES = S // BANK
 BANK_BYTES = 4 * BANK
 SLOT_BYTES = 4 * S
 RING = 3
+POOL_COLS = 512
 ABS_SLOT, W1_SLOT, X_SLOT = 0, 1, 2
 COS_SLOT = 3
 SUM_SLOT = COS_SLOT + RING
@@ -167,7 +168,11 @@ def tile_list_lens_edge_refiner_kernel(
             if i > 0:
                 pick(*divmod(i - 1, PACK))
             h[g, t] = keep.tile([P, S], F32, name=f"h{g}{t}")
-            nc.vector.scalar_tensor_tensor(h[g, t][:], cosb[:], gain_sb[:, g, t : t + 1], summ[:], ALU.mult, ALU.mult)
+            lo, hi = slice(0, POOL_COLS), slice(POOL_COLS, S)
+            gain_col = gain_sb[:, g, t : t + 1]
+            nc.gpsimd.tensor_scalar(cosb[:, lo], cosb[:, lo], gain_col, 0.0, ALU.mult, ALU.add)
+            nc.gpsimd.tensor_tensor(h[g, t][:, lo], cosb[:, lo], summ[:, lo], ALU.mult)
+            nc.vector.scalar_tensor_tensor(h[g, t][:, hi], cosb[:, hi], gain_col, summ[:, hi], ALU.mult, ALU.mult)
 
         def pick(g, t):
             nc.vector.tensor_copy(picked[g][:, t, 0:E], h[g, t][:].indirect(pos_sb[:]))

import math
from contextlib import ExitStack

import concourse.mybir as mybir

K, T, S, H, E = 512, 4096, 1024, 1024, 512
FLOPS = 2 * (2 * K * H * S + H * H * E)

F32 = mybir.dt.float32
BF16 = mybir.dt.bfloat16
I32 = mybir.dt.int32
U32 = mybir.dt.uint32
U16 = mybir.dt.uint16
U8 = mybir.dt.uint8
FP8X4 = mybir.dt.float8_e4m3fn_x4
FP4X4 = mybir.dt.float4_e2m1fn_x4
ACT = mybir.ActivationFunctionType
ALU = mybir.AluOpType

P = 128
PACK = 4
GROUP = P * PACK
BANK = 512
GROUPS = H // GROUP
HALVES = S // BANK
BANK_BYTES = 4 * BANK
SLOT_BYTES = 4 * S
RING = 3
POOL_COLS = 512
ABS_SLOT, W1_SLOT, X_SLOT = 0, 1, 2
COS_SLOT = 3
SUM_SLOT = COS_SLOT + RING
PICK_SLOT = SUM_SLOT + RING
A_BANKS, B_BANKS = 2, 6


def tile_list_lens_edge_refiner_kernel(
    tc, tab_words, tab_scales, offs, w1, w4_words, w4_scales, gain, pos1, base, w2, skip, wgo, out
):
    nc = tc.nc
    with ExitStack() as ctx:
        keep = ctx.enter_context(tc.tile_pool(name="keep", bufs=1))
        work = ctx.enter_context(tc.tile_pool(name="work", bufs=2))
        psum = ctx.enter_context(tc.psum_pool(name="psum", bufs=1))
        slots = ctx.enter_context(tc.tile_pool(name="slots", bufs=1))

        def in_slot(slot, shape, dtype, name):
            return slots.tile(shape, dtype, name=name, offset=slot * SLOT_BYTES, align_bytes=64)

        def in_bank(bank, width, name):
            return psum.tile([P, width], F32, name=name, offset=bank * BANK_BYTES)


        offs_sb = keep.tile([P, S // 16], U16, name="offs_sb")
        pos_sb = keep.tile([P, E // 16], U16, name="pos_sb")
        tab_w = keep.tile([P, T], U32, name="tab_w", align_bytes=64)
        tab_s = keep.tile([P, T], U8, name="tab_s", align_bytes=64)
        w4_raw = keep.tile([P, 2 * H], U8, name="w4_raw", align_bytes=64)
        w4s_raw = keep.tile([P, H], U8, name="w4s_raw", align_bytes=64)
        w4_c = keep.tile([P, 2 * H], U8, name="w4_c", align_bytes=64)
        w4_s = keep.tile([P, H], U8, name="w4_s", align_bytes=64)
        gain_sb = keep.tile([P, GROUPS, PACK], F32, name="gain_sb")
        skip_sb = keep.tile([P, GROUPS, PACK], F32, name="skip_sb")
        wgo_sb = keep.tile([P, PACK, E], F32, name="wgo_sb")

        nc.gpsimd.memset(w4s_raw[:].bitcast(I32), 0)
        warm_in = keep.tile([P, 1], F32, name="warm_in")
        warm_out = keep.tile([P, 1], F32, name="warm_out")
        nc.gpsimd.memset(warm_in[:], 0.0)
        nc.scalar.activation(warm_out[:], warm_in[:], ACT.Silu)

        nc.vector.memset(tab_s[:].bitcast(I32), 0)

        def load_rows(src, tag, bufs):
            raw = work.tile([P, PACK, BANK], F32, name=tag, tag=tag, bufs=bufs)
            nc.sync.dma_start(raw[:], src.rearrange("(p j) c -> p j c", j=PACK))
            return raw

        for q in range(4):
            nc.sync.dma_start(w4s_raw[32 * q : 32 * q + 4, :].bitcast(I32), w4_scales[0, 4 * q : 4 * q + 4, :].bitcast(I32))
        w1_raw = [load_rows(w1[:, 0:GROUP], "w_raw", 4)]
        nc.sync.dma_start(offs_sb[:], offs)
        for q in range(4):
            nc.sync.dma_start(tab_s[32 * q : 32 * q + 4, :].bitcast(I32), tab_scales[0, 4 * q : 4 * q + 4, :].bitcast(I32))
        nc.sync.dma_start(w4_raw[:].bitcast(I32), w4_words[0].bitcast(I32))
        nc.sync.dma_start(tab_w[:].bitcast(I32), tab_words[0].rearrange("p t i -> p (t i)").bitcast(I32))
        w1_raw.append(load_rows(w1[:, GROUP : 2 * GROUP], "w_raw", 4))
        nc.sync.dma_start(gain_sb[:], gain.rearrange("(g p t) -> p g t", g=GROUPS, t=PACK))
        nc.sync.dma_start(pos_sb[:], pos1)
        base_sb = [load_rows(base[g * GROUP : (g + 1) * GROUP, :], "base_sb", 2) for g in range(GROUPS)]
        w2_raw = {}
        for g in range(GROUPS):
            for a in range(GROUPS):
                w2_raw[g, a] = load_rows(w2[a * GROUP : (a + 1) * GROUP, g * GROUP : (g + 1) * GROUP], "w_raw", 4)
        nc.sync.dma_start(skip_sb[:], skip.rearrange("(g p t) -> p g t", g=GROUPS, t=PACK))
        for u in range(4):
            nc.sync.dma_start(wgo_sb[32 * u : 32 * u + 32], wgo.rearrange("(p t) m -> p t m", t=PACK))

        v_w = [keep.tile([P, BANK], U32, name=f"v_w{c}", align_bytes=64) for c in range(HALVES)]
        v_s = [keep.tile([P, BANK], U8, name=f"v_s{c}", align_bytes=64) for c in range(HALVES)]
        cols = BANK // 16
        for c in range(HALVES):
            nc.vector.tensor_copy(v_s[c][:], tab_s[:].indirect(offs_sb[:, c * cols : (c + 1) * cols]))
        nc.vector.tensor_copy(
            w4_c[:].bitcast(U16).rearrange("p (g t m) -> p g m t", g=GROUPS, t=PACK),
            w4_raw[:].bitcast(U16).rearrange("p (g m t) -> p g m t", g=GROUPS, t=PACK),
        )
        nc.vector.tensor_copy(
            w4_s[:].rearrange("p (g t m) -> p g t m", g=GROUPS, t=PACK),
            w4s_raw[:].rearrange("p (g m t) -> p g t m", g=GROUPS, t=PACK),
        )
        for c in range(HALVES):
            nc.vector.tensor_copy(v_w[c][:], tab_w[:].indirect(offs_sb[:, c * cols : (c + 1) * cols]))

        def round_weight(raw, slot, name, copy=nc.scalar.copy):
            grouped = in_slot(slot, [P, GROUP * PACK], BF16, name)
            dst = grouped[:].rearrange("p (t m j) -> p m j t", t=PACK, j=PACK)
            src = raw[:].rearrange("p j (m t) -> p m j t", t=PACK)
            copy(dst, src)
            return grouped

        def mx_tiles(name):
            codes = keep.tile([P, BANK], U32, name=name + "_c", align_bytes=64)
            scales = keep.tile([P, BANK], U8, name=name + "_s", align_bytes=64)
            return codes, scales

        def quantize_columns(grouped, dst, m):
            codes, scales = dst
            nc.vector.quantize_mx(out=codes[:, m].bitcast(FP8X4), scales=scales[:, m], in_=grouped[:, PACK * m.start : PACK * m.stop])

        def quantize(grouped, name):
            dst = mx_tiles(name)
            quantize_columns(grouped, dst, slice(0, BANK))
            return dst

        w1_q = {0: quantize(round_weight(w1_raw[0], W1_SLOT, "w1g0"), "w1q0")}
        w2_q = {}
        x_q = {}
        h = {}
        picked = {}

        def features(g, t):
            w1_c, w1_s = w1_q[g]
            m = slice(t * P, (t + 1) * P)
            n0 = g * GROUP + t * P
            i = g * PACK + t
            if i == 0:
                absb = in_slot(ABS_SLOT, [P, S], F32, "abs0")
            else:
                gp, tp = divmod(i - 1, PACK)
                if tp == 0:
                    picked[gp] = in_slot(PICK_SLOT + PACK * gp, [P, PACK, S], F32, f"picked{gp}")
                absb = picked[gp][:, tp, :]
            cosb = in_slot(COS_SLOT + i % RING, [P, S], F32, f"cos{i}")
            summ = in_slot(SUM_SLOT + i % RING, [P, S], F32, f"sum{i}")
            for c in range(HALVES):
                j = slice(c * BANK, (c + 1) * BANK)
                b_ps = in_bank(A_BANKS + (HALVES * i + c) % B_BANKS, BANK, f"b{i}{c}")
                a_ps = in_bank(c, BANK, f"a{i}{c}")
                nc.tensor.matmul_mx(b_ps[:], lhsT=w4_c[:, 2 * n0 : 2 * (n0 + P)].bitcast(FP4X4), lhsT_scale=w4_s[:, n0 : n0 + P],
                                    rhs=v_w[c][:].bitcast(FP8X4), rhs_scale=v_s[c][:], start=True, stop=True)
                nc.tensor.matmul_mx(a_ps[:], lhsT=w1_c[:, m].bitcast(FP8X4), lhsT_scale=w1_s[:, m],
                                    rhs=v_w[c][:].bitcast(FP8X4), rhs_scale=v_s[c][:], start=True, stop=True)
                nc.scalar.activation(absb[:, j], b_ps[:], ACT.Abs)
                nc.scalar.activation(summ[:, j], a_ps[:], ACT.Tanh)
                nc.vector.tensor_tensor(summ[:, j], b_ps[:], summ[:, j], ALU.add)
            nc.scalar.activation(cosb[:], absb[:, :], ACT.Sin, bias=math.pi / 2, scale=-1.0)
            if i > 0:
                pick(*divmod(i - 1, PACK))
            h[g, t] = keep.tile([P, S], F32, name=f"h{g}{t}")
            lo, hi = slice(0, POOL_COLS), slice(POOL_COLS, S)
            gain_col = gain_sb[:, g, t : t + 1]
            nc.gpsimd.tensor_scalar(cosb[:, lo], cosb[:, lo], gain_col, 0.0, ALU.mult, ALU.add)
            nc.gpsimd.tensor_tensor(h[g, t][:, lo], cosb[:, lo], summ[:, lo], ALU.mult)
            nc.vector.scalar_tensor_tensor(h[g, t][:, hi], cosb[:, hi], gain_col, summ[:, hi], ALU.mult, ALU.mult)

        def pick(g, t):
            nc.vector.tensor_copy(picked[g][:, t, 0:E], h[g, t][:].indirect(pos_sb[:]))

        def edge_operand(g, parts):
            grouped = in_slot(X_SLOT, [P, E * PACK], BF16, f"xg{g}")
            x_q[g] = mx_tiles(f"xq{g}")
            for m in parts:
                nc.vector.tensor_tensor(
                    grouped[:, PACK * m.start : PACK * m.stop].rearrange("p (c i t) -> p c t i", i=2, t=PACK),
                    picked[g][:, :, m].rearrange("p t (c i) -> p c t i", i=2),
                    base_sb[g][:, :, m].rearrange("p t (c i) -> p c t i", i=2),
                    ALU.max,
                )
                quantize_columns(grouped, x_q[g], m)

        whole = [slice(0, E)]
        halves = [slice(0, E // 2), slice(E // 2, E)]
        tiles = [(g, t) for g in range(GROUPS) for t in range(PACK)]
        w_grouped = {}
        for i, (g, t) in enumerate(tiles):
            features(g, t)
            if i == 0:
                w_grouped["w1"] = round_weight(w1_raw[1], W1_SLOT, "w1g1", nc.vector.tensor_copy)
            if i == 1:
                w1_q[1] = quantize(w_grouped["w1"], "w1q1")
            if i == 4:
                edge_operand(0, whole)
                w_grouped[0, 0] = round_weight(w2_raw[0, 0], PICK_SLOT, "w2g00")
            if i == 6:
                w2_q[0, 0] = quantize(w_grouped[0, 0], "w2q00")
        w_grouped[0, 1] = round_weight(w2_raw[0, 1], COS_SLOT, "w2g01")
        pick(*tiles[-1])
        w2_q[0, 1] = quantize(w_grouped[0, 1], "w2q01")
        edge_operand(1, halves)

        next_bank = [0, 1, 4, 5, 0, 1, 4, 5, 0]
        for i, (g, t) in enumerate(tiles):
            n = slice(t * P, (t + 1) * P)
            page = in_slot((COS_SLOT, SUM_SLOT)[i % 2] + (1 + i // 2) % RING, [P, S], F32, f"page{i}")
            nc.scalar.activation(page[:], h[g, t][:], ACT.Copy, scale=skip_sb[:, g, t : t + 1])
            for m in halves if i == 0 else whole:
                width = m.stop - m.start
                y_ps = in_bank(next_bank.pop(0), width, f"y{i}_{m.start}")
                for a in range(GROUPS):
                    w2_c, w2_s = w2_q[g, a]
                    x_c, x_s = x_q[a]
                    nc.tensor.matmul_mx(y_ps[:], lhsT=w2_c[:, n].bitcast(FP8X4), lhsT_scale=w2_s[:, n],
                                        rhs=x_c[:, m].bitcast(FP8X4), rhs_scale=x_s[:, m], start=(a == 0), stop=(a == GROUPS - 1))
                y = work.tile([P, width], F32, name="y", bufs=3)
                nc.scalar.activation(y[:], y_ps[:], ACT.Tanh)
                nc.vector.tensor_tensor(page[:].indirect(pos_sb[:, m.start // 16 : m.stop // 16]), y[:], wgo_sb[:, t, m], ALU.mult)
            if i in (0, 1):
                w_grouped[1, i] = round_weight(w2_raw[1, i], PICK_SLOT + PACK + i, f"w2g1{i}")
            if i in (1, 2):
                w2_q[1, i - 1] = quantize(w_grouped[1, i - 1], f"w2q1{i - 1}")
            rows = out[g * GROUP : (g + 1) * GROUP, :].rearrange("(p t) j -> p t j", t=PACK)
            nc.sync.dma_start(rows[:, t, :], page[:])
